import numpy as np
CORES = [3,11,19,27,35,43,51,59,67,75,83,91,99,107,115,123,131,139,147,155,163,171,179,187,195,203,211,219,227,235,243,251]
N = 32
WIDTHS = [1024 if r == 9 else 64 if r == 20 else 32 for r in range(N)]
WMAX = 1024
def setup_inputs(rng):
    return {"x": rng.standard_normal((N, 128, 2048), dtype=np.float32)}
def reference(x):
    s = x.sum(axis=0, dtype=np.float64).astype(x.dtype)
    y = np.full((N, 128, WMAX), np.nan, x.dtype)
    o = 0
    for r in range(N):
        y[r][:, :WIDTHS[r]] = s[:, o:o + WIDTHS[r]]
        o += WIDTHS[r]
    return {"y": y}

@@ -1,0 +1,85 @@
+from concourse.mybir import AluOpType
+
+SCRATCH = {
+    "lo": ("sbuf", [128, 32, 64], "float32"),
+    "lh": ("sbuf", [128, 32, 34], "float32"),
+    "xs": ("sbuf", [128, 2048], "float32"),
+    "l9": ("sbuf", [128, 1024], "float32"),
+}
+SEMAPHORES = ["ld", "own", "hot", "fin", "snt", "acc"]
+
+
+def plan(widths):
+    n = len(widths)
+    off = [sum(widths[:r]) for r in range(n)]
+    own = [(off[r], widths[r]) for r in range(n)]
+    own[9] = (off[9], 32)
+    hot = [None] * n
+    pos = off[9] + 32
+    k = 0
+    for r in range(n):
+        if r in (9, 20):
+            continue
+        w = 34 if k < 2 else 33
+        k += 1
+        hot[r] = (pos, w)
+        pos += w
+    return off, own, hot
+
+
+def rank_program(g, core, T, topo):
+    r = T.rank_of(core)
+    if r is None:
+        return
+    widths = T.tables["WIDTHS"]
+    off, own, hot = plan(widths)
+    n = len(widths)
+    S = T.sem
+    g.dma_start(T.xs[:], T.x[:]).then_inc(S.ld, 16)
+    o, w = own[r]
+    g.dma_start(T.lo[:, r, 0:w], T.x[:, o:o + w]).then_inc(S.ld, 16)
+    nld = 32
+    if hot[r]:
+        ho, hw = hot[r]
+        g.dma_start(T.lh[:, r, 0:hw], T.x[:, ho:ho + hw]).then_inc(S.ld, 16)
+        nld += 16
+    g.wait_ge(S.ld, nld)
+    sent = 0
+    for d in range(1, n):
+        q = (r + d) % n
+        dst = T.cores[q]
+        rid, pid = topo.addr(dst, core)
+        qo, qw = own[q]
+        g.remote_dma(T.lo[:, r, 0:qw], T.xs[:, qo:qo + qw], S.own, S.snt, pid, rid, 0xFF)
+        sent += 8
+        if hot[q]:
+            qo, qw = hot[q]
+            g.remote_dma(T.lh[:, r, 0:qw], T.xs[:, qo:qo + qw], S.hot, S.snt, pid, rid, 0xFF)
+            sent += 8
+    acc = 0
+    if hot[r]:
+        g.wait_ge(S.hot, 8 * (n - 1))
+        h = n // 2
+        while h >= 1:
+            g.dma_start(T.lh[:, 0:h, 0:hw], T.lh[:, h:2 * h, 0:hw], accum_op=AluOpType.add).then_inc(S.acc, 16)
+            acc += 16
+            g.wait_ge(S.acc, acc)
+            h //= 2
+        rid, pid = topo.addr(T.cores[9], core)
+        g.remote_dma(T.l9[:, ho - off[9]:ho - off[9] + hw], T.lh[:, 0, 0:hw], S.fin, S.snt, pid, rid, 0xFF)
+        sent += 8
+    g.wait_ge(S.own, 8 * (n - 1))
+    h = n // 2
+    while h >= 1:
+        g.dma_start(T.lo[:, 0:h, 0:w], T.lo[:, h:2 * h, 0:w], accum_op=AluOpType.add).then_inc(S.acc, 16)
+        acc += 16
+        g.wait_ge(S.acc, acc)
+        h //= 2
+    g.dma_start(T.y[:, 0:w], T.lo[:, 0, 0:w]).then_inc(S.acc, 16)
+    acc += 16
+    if r == 9:
+        g.wait_ge(S.fin, 8 * 30)
+        g.dma_start(T.y[:, 32:1024], T.l9[:, 32:1024]).then_inc(S.acc, 16)
+        acc += 16
+    g.wait_ge(S.acc, acc)
+    g.wait_ge(S.snt, sent)

@@ -1,12 +1,13 @@
-from concourse.mybir import AluOpType
+from concourse.bass import DstId, RemoteDMATransfer
 
 SCRATCH = {
     "lo": ("sbuf", [128, 32, 64], "float32"),
     "lh": ("sbuf", [128, 32, 34], "float32"),
     "xs": ("sbuf", [128, 2048], "float32"),
     "l9": ("sbuf", [128, 1024], "float32"),
+    "res": ("sbuf", [128, 64], "float32"),
 }
-SEMAPHORES = ["ld", "own", "hot", "fin", "snt", "acc"]
+SEMAPHORES = ["ld", "own", "hot", "fin", "snt", "rs", "acc"]
 
 
 def plan(widths):
@@ -27,56 +28,56 @@ def plan(widths):
     return off, own, hot
 
 
+def fold(g, srcs, dst, dst_core, core, topo, sem, local_sem, mask):
+    rid, pid = topo.addr(dst_core, core)
+    g.remote_dma_fused([RemoteDMATransfer(dst_ids=[DstId(rid=rid, pnc=pid)], dma_engine_mask=mask, remote_sem=sem,
+                                          srcs=srcs, dsts=[dst], alu_op=1)], local_sem=local_sem)
+
+
 def rank_program(g, core, T, topo):
-    r = T.rank_of(core)
-    if r is None:
-        return
     widths = T.tables["WIDTHS"]
     off, own, hot = plan(widths)
     n = len(widths)
     S = T.sem
+    r = T.rank_of(core)
+    if r is None:
+        r = T.rank_of(core + 1)
+        if r is None or core % 8 != 2:
+            return
+        o, w = own[r]
+        g.wait_ge(S.own, 8 * n)
+        fold(g, [T.lo[:, k, 0:w] for k in range(n)], T.res[:, 0:w], core + 1, core, topo, S.rs, S.snt, 0xFFFF)
+        g.wait_ge(S.snt, 16)
+        return
     g.dma_start(T.xs[:], T.x[:]).then_inc(S.ld, 16)
-    o, w = own[r]
-    g.dma_start(T.lo[:, r, 0:w], T.x[:, o:o + w]).then_inc(S.ld, 16)
-    nld = 32
+    nld = 16
     if hot[r]:
         ho, hw = hot[r]
         g.dma_start(T.lh[:, r, 0:hw], T.x[:, ho:ho + hw]).then_inc(S.ld, 16)
         nld += 16
     g.wait_ge(S.ld, nld)
     sent = 0
-    for d in range(1, n):
+    for d in range(1, n + 1):
         q = (r + d) % n
         dst = T.cores[q]
-        rid, pid = topo.addr(dst, core)
+        rid, pid = topo.addr(dst - 1, core)
         qo, qw = own[q]
         g.remote_dma(T.lo[:, r, 0:qw], T.xs[:, qo:qo + qw], S.own, S.snt, pid, rid, 0xFF)
         sent += 8
-        if hot[q]:
+        if hot[q] and q != r:
+            rid, pid = topo.addr(dst, core)
             qo, qw = hot[q]
             g.remote_dma(T.lh[:, r, 0:qw], T.xs[:, qo:qo + qw], S.hot, S.snt, pid, rid, 0xFF)
             sent += 8
-    acc = 0
     if hot[r]:
         g.wait_ge(S.hot, 8 * (n - 1))
-        h = n // 2
-        while h >= 1:
-            g.dma_start(T.lh[:, 0:h, 0:hw], T.lh[:, h:2 * h, 0:hw], accum_op=AluOpType.add).then_inc(S.acc, 16)
-            acc += 16
-            g.wait_ge(S.acc, acc)
-            h //= 2
-        rid, pid = topo.addr(T.cores[9], core)
-        g.remote_dma(T.l9[:, ho - off[9]:ho - off[9] + hw], T.lh[:, 0, 0:hw], S.fin, S.snt, pid, rid, 0xFF)
+        fold(g, [T.lh[:, k, 0:hw] for k in range(n)], T.l9[:, ho - off[9]:ho - off[9] + hw], T.cores[9], core, topo,
+             S.fin, S.snt, 0xFF)
         sent += 8
-    g.wait_ge(S.own, 8 * (n - 1))
-    h = n // 2
-    while h >= 1:
-        g.dma_start(T.lo[:, 0:h, 0:w], T.lo[:, h:2 * h, 0:w], accum_op=AluOpType.add).then_inc(S.acc, 16)
-        acc += 16
-        g.wait_ge(S.acc, acc)
-        h //= 2
-    g.dma_start(T.y[:, 0:w], T.lo[:, 0, 0:w]).then_inc(S.acc, 16)
-    acc += 16
+    o, w = own[r]
+    g.wait_ge(S.rs, 16)
+    g.dma_start(T.y[:, 0:w], T.res[:, 0:w]).then_inc(S.acc, 16)
+    acc = 16
     if r == 9:
         g.wait_ge(S.fin, 8 * 30)
         g.dma_start(T.y[:, 32:1024], T.l9[:, 32:1024]).then_inc(S.acc, 16)

@@ -1,86 +1,71 @@
 from concourse.bass import DstId, RemoteDMATransfer
 
 SCRATCH = {
-    "lo": ("sbuf", [128, 32, 64], "float32"),
-    "lh": ("sbuf", [128, 32, 34], "float32"),
+    "slot": ("sbuf", [128, 32, 32], "float32"),
     "xs": ("sbuf", [128, 2048], "float32"),
     "l9": ("sbuf", [128, 1024], "float32"),
     "res": ("sbuf", [128, 64], "float32"),
 }
-SEMAPHORES = ["ld", "own", "hot", "fin", "snt", "rs", "acc"]
+SEMAPHORES = ["ld", "arr", "fin", "snt", "acc"]
+HOT, WIDE = 9, 20
 
 
 def plan(widths):
     n = len(widths)
     off = [sum(widths[:r]) for r in range(n)]
-    own = [(off[r], widths[r]) for r in range(n)]
-    own[9] = (off[9], 32)
-    hot = [None] * n
-    pos = off[9] + 32
-    k = 0
-    for r in range(n):
-        if r in (9, 20):
-            continue
-        w = 34 if k < 2 else 33
-        k += 1
-        hot[r] = (pos, w)
-        pos += w
-    return off, own, hot
+    a = [off[HOT] + 32 * q for q in range(n)]
+    b = [off[q] for q in range(n)]
+    bdst = [(q, 0) for q in range(n)]
+    b[HOT] = off[WIDE] + 32
+    bdst[HOT] = (WIDE, 32)
+    return off, a, b, bdst
 
 
-def fold(g, srcs, dst, dst_core, core, topo, sem, local_sem, mask):
+def xfer(topo, core, dst_core, mask, sem, srcs, dst):
     rid, pid = topo.addr(dst_core, core)
-    g.remote_dma_fused([RemoteDMATransfer(dst_ids=[DstId(rid=rid, pnc=pid)], dma_engine_mask=mask, remote_sem=sem,
-                                          srcs=srcs, dsts=[dst], alu_op=1)], local_sem=local_sem)
+    return RemoteDMATransfer(dst_ids=[DstId(rid=rid, pnc=pid)], dma_engine_mask=mask, remote_sem=sem,
+                             srcs=srcs, dsts=[dst], alu_op=1 if len(srcs) > 1 else 0)
 
 
 def rank_program(g, core, T, topo):
     widths = T.tables["WIDTHS"]
-    off, own, hot = plan(widths)
+    off, a, b, bdst = plan(widths)
     n = len(widths)
     S = T.sem
-    r = T.rank_of(core)
+    base = core - core % 8
+    r = T.rank_of(base + 3)
     if r is None:
-        r = T.rank_of(core + 1)
-        if r is None or core % 8 != 2:
-            return
-        o, w = own[r]
-        g.wait_ge(S.own, 8 * n)
-        fold(g, [T.lo[:, k, 0:w] for k in range(n)], T.res[:, 0:w], core + 1, core, topo, S.rs, S.snt, 0xFFFF)
-        g.wait_ge(S.snt, 16)
+        return
+    c = core % 8
+    if c in (2, 6):
+        g.wait_ge(S.arr, n)
+        srcs = [T.slot[:, k, :] for k in range(n)]
+        if c == 2:
+            t = xfer(topo, core, T.cores[HOT], 0xFF, S.fin, srcs, T.l9[:, 32 * r:32 * r + 32])
+        else:
+            q, col = bdst[r]
+            t = xfer(topo, core, T.cores[q], 0xFF, S.fin, srcs, T.res[:, col:col + 32])
+        g.remote_dma_fused([t], local_sem=S.snt)
+        g.wait_ge(S.snt, 8)
+        return
+    if c != 3:
         return
     g.dma_start(T.xs[:], T.x[:]).then_inc(S.ld, 16)
-    nld = 16
-    if hot[r]:
-        ho, hw = hot[r]
-        g.dma_start(T.lh[:, r, 0:hw], T.x[:, ho:ho + hw]).then_inc(S.ld, 16)
-        nld += 16
-    g.wait_ge(S.ld, nld)
-    sent = 0
-    for d in range(1, n + 1):
-        q = (r + d) % n
-        dst = T.cores[q]
-        rid, pid = topo.addr(dst - 1, core)
-        qo, qw = own[q]
-        g.remote_dma(T.lo[:, r, 0:qw], T.xs[:, qo:qo + qw], S.own, S.snt, pid, rid, 0xFF)
-        sent += 8
-        if hot[q] and q != r:
-            rid, pid = topo.addr(dst, core)
-            qo, qw = hot[q]
-            g.remote_dma(T.lh[:, r, 0:qw], T.xs[:, qo:qo + qw], S.hot, S.snt, pid, rid, 0xFF)
-            sent += 8
-    if hot[r]:
-        g.wait_ge(S.hot, 8 * (n - 1))
-        fold(g, [T.lh[:, k, 0:hw] for k in range(n)], T.l9[:, ho - off[9]:ho - off[9] + hw], T.cores[9], core, topo,
-             S.fin, S.snt, 0xFF)
-        sent += 8
-    o, w = own[r]
-    g.wait_ge(S.rs, 16)
-    g.dma_start(T.y[:, 0:w], T.res[:, 0:w]).then_inc(S.acc, 16)
-    acc = 16
-    if r == 9:
-        g.wait_ge(S.fin, 8 * 30)
-        g.dma_start(T.y[:, 32:1024], T.l9[:, 32:1024]).then_inc(S.acc, 16)
-        acc += 16
-    g.wait_ge(S.acc, acc)
-    g.wait_ge(S.snt, sent)
+    g.wait_ge(S.ld, 16)
+    jobs = []
+    for col, helper in ((a, 2), (b, 6)):
+        for d in range(1, n + 1):
+            q = (r + d) % n
+            jobs.append((T.cores[q] - 3 + helper, col[q]))
+    for i in range(0, len(jobs), 8):
+        g.remote_dma_fused([xfer(topo, core, dc, 1 << e, S.arr, [T.xs[:, o:o + 32]], T.slot[:, r, :])
+                            for e, (dc, o) in enumerate(jobs[i:i + 8])], local_sem=S.snt)
+    if r == HOT:
+        g.wait_ge(S.fin, 8 * n)
+        g.dma_start(T.y[:, 0:1024], T.l9[:]).then_inc(S.acc, 16)
+    else:
+        w = widths[r]
+        g.wait_ge(S.fin, 8 * (w // 32))
+        g.dma_start(T.y[:, 0:w], T.res[:, 0:w]).then_inc(S.acc, 16)
+    g.wait_ge(S.acc, 16)
+    g.wait_ge(S.snt, len(jobs))

@@ -3,22 +3,23 @@ from concourse.bass import DstId, RemoteDMATransfer
 SCRATCH = {
     "slot": ("sbuf", [128, 32, 32], "float32"),
     "xs": ("sbuf", [128, 2048], "float32"),
-    "l9": ("sbuf", [128, 1024], "float32"),
     "res": ("sbuf", [128, 64], "float32"),
+    "dh": ("dram", [32, 128, 32], "float32"),
+    "sd": ("dram", [32, 128, 32], "float32"),
+    "f9": ("dram", [32, 128, 32], "float32"),
 }
-SEMAPHORES = ["ld", "arr", "fin", "snt", "acc"]
+SEMAPHORES = ["lda", "ldb", "arr", "fin", "snt", "acc"]
 HOT, WIDE = 9, 20
 
 
 def plan(widths):
     n = len(widths)
     off = [sum(widths[:r]) for r in range(n)]
-    a = [off[HOT] + 32 * q for q in range(n)]
     b = [off[q] for q in range(n)]
     bdst = [(q, 0) for q in range(n)]
     b[HOT] = off[WIDE] + 32
     bdst[HOT] = (WIDE, 32)
-    return off, a, b, bdst
+    return off, b, bdst
 
 
 def xfer(topo, core, dst_core, mask, sem, srcs, dst):
@@ -29,7 +30,7 @@ def xfer(topo, core, dst_core, mask, sem, srcs, dst):
 
 def rank_program(g, core, T, topo):
     widths = T.tables["WIDTHS"]
-    off, a, b, bdst = plan(widths)
+    off, b, bdst = plan(widths)
     n = len(widths)
     S = T.sem
     base = core - core % 8
@@ -39,33 +40,35 @@ def rank_program(g, core, T, topo):
     c = core % 8
     if c in (2, 6):
         g.wait_ge(S.arr, n)
-        srcs = [T.slot[:, k, :] for k in range(n)]
         if c == 2:
-            t = xfer(topo, core, T.cores[HOT], 0xFF, S.fin, srcs, T.l9[:, 32 * r:32 * r + 32])
+            t = xfer(topo, core, T.cores[HOT], 0xFF, S.fin, [T.sd[k] for k in range(n)], T.f9[r])
         else:
             q, col = bdst[r]
-            t = xfer(topo, core, T.cores[q], 0xFF, S.fin, srcs, T.res[:, col:col + 32])
+            t = xfer(topo, core, T.cores[q], 0xFF, S.fin, [T.slot[:, k, :] for k in range(n)], T.res[:, col:col + 32])
         g.remote_dma_fused([t], local_sem=S.snt)
         g.wait_ge(S.snt, 8)
         return
     if c != 3:
         return
-    g.dma_start(T.xs[:], T.x[:]).then_inc(S.ld, 16)
-    g.wait_ge(S.ld, 16)
-    jobs = []
-    for col, helper in ((a, 2), (b, 6)):
-        for d in range(1, n + 1):
-            q = (r + d) % n
-            jobs.append((T.cores[q] - 3 + helper, col[q]))
-    for i in range(0, len(jobs), 8):
-        g.remote_dma_fused([xfer(topo, core, dc, 1 << e, S.arr, [T.xs[:, o:o + 32]], T.slot[:, r, :])
-                            for e, (dc, o) in enumerate(jobs[i:i + 8])], local_sem=S.snt)
+    h0, h1 = off[HOT], off[HOT] + widths[HOT]
+    g.dma_start(T.dh[:], T.x[:, h0:h1]).then_inc(S.lda, 16)
+    g.dma_start(T.xs[:, 0:h0], T.x[:, 0:h0]).then_inc(S.ldb, 16)
+    g.dma_start(T.xs[:, h1:], T.x[:, h1:]).then_inc(S.ldb, 16)
+    order = [(r + d) % n for d in range(1, n + 1)]
+    g.wait_ge(S.lda, 16)
+    for i in range(0, n, 8):
+        g.remote_dma_fused([xfer(topo, core, T.cores[q] - 1, 1 << e, S.arr, [T.dh[q]], T.sd[r])
+                            for e, q in enumerate(order[i:i + 8])], local_sem=S.snt)
+    g.wait_ge(S.ldb, 32)
+    for i in range(0, n, 8):
+        g.remote_dma_fused([xfer(topo, core, T.cores[q] + 3, 1 << e, S.arr, [T.xs[:, b[q]:b[q] + 32]], T.slot[:, r, :])
+                            for e, q in enumerate(order[i:i + 8])], local_sem=S.snt)
     if r == HOT:
         g.wait_ge(S.fin, 8 * n)
-        g.dma_start(T.y[:, 0:1024], T.l9[:]).then_inc(S.acc, 16)
+        g.dma_start(T.y[:, 0:1024], T.f9[:]).then_inc(S.acc, 16)
     else:
         w = widths[r]
         g.wait_ge(S.fin, 8 * (w // 32))
         g.dma_start(T.y[:, 0:w], T.res[:, 0:w]).then_inc(S.acc, 16)
     g.wait_ge(S.acc, 16)
-    g.wait_ge(S.snt, len(jobs))
+    g.wait_ge(S.snt, 2 * n)

@@ -2,13 +2,13 @@ from concourse.bass import DstId, RemoteDMATransfer
 
 SCRATCH = {
     "slot": ("sbuf", [128, 32, 32], "float32"),
-    "xs": ("sbuf", [128, 2048], "float32"),
+    "xb": ("sbuf", [128, 1024], "float32"),
     "res": ("sbuf", [128, 64], "float32"),
     "dh": ("dram", [32, 128, 32], "float32"),
     "sd": ("dram", [32, 128, 32], "float32"),
     "f9": ("dram", [32, 128, 32], "float32"),
 }
-SEMAPHORES = ["lda", "ldb", "arr", "fin", "snt", "acc"]
+SEMAPHORES = ["lda", "ldb", "arr", "fin", "snt", "acc", "got"]
 HOT, WIDE = 9, 20
 
 
@@ -19,7 +19,12 @@ def plan(widths):
     bdst = [(q, 0) for q in range(n)]
     b[HOT] = off[WIDE] + 32
     bdst[HOT] = (WIDE, 32)
+    b = [o if o < off[HOT] else o - widths[HOT] for o in b]
     return off, b, bdst
+
+
+def a_core(q):
+    return 2 if q % 4 < 2 else 6
 
 
 def xfer(topo, core, dst_core, mask, sem, srcs, dst):
@@ -38,9 +43,10 @@ def rank_program(g, core, T, topo):
     if r is None:
         return
     c = core % 8
+    order = [(r + d) % n for d in range(1, n + 1)]
     if c in (2, 6):
         g.wait_ge(S.arr, n)
-        if c == 2:
+        if c == a_core(r):
             t = xfer(topo, core, T.cores[HOT], 0xFF, S.fin, [T.sd[k] for k in range(n)], T.f9[r])
         else:
             q, col = bdst[r]
@@ -48,20 +54,26 @@ def rank_program(g, core, T, topo):
         g.remote_dma_fused([t], local_sem=S.snt)
         g.wait_ge(S.snt, 8)
         return
+    if c == 7:
+        g.wait_ge(S.got, 16)
+        for i in range(0, n, 8):
+            g.remote_dma_fused([xfer(topo, core, T.cores[q] - 3 + 8 - a_core(q), 1 << e, S.arr,
+                                     [T.xb[:, b[q]:b[q] + 32]], T.slot[:, r, :])
+                                for e, q in enumerate(order[i:i + 8])], local_sem=S.snt)
+        g.wait_ge(S.snt, n)
+        return
     if c != 3:
         return
     h0, h1 = off[HOT], off[HOT] + widths[HOT]
+    g.dma_start(T.xb[:, 0:h0], T.x[:, 0:h0]).then_inc(S.ldb, 16)
+    g.dma_start(T.xb[:, h0:], T.x[:, h1:]).then_inc(S.ldb, 16)
     g.dma_start(T.dh[:], T.x[:, h0:h1]).then_inc(S.lda, 16)
-    g.dma_start(T.xs[:, 0:h0], T.x[:, 0:h0]).then_inc(S.ldb, 16)
-    g.dma_start(T.xs[:, h1:], T.x[:, h1:]).then_inc(S.ldb, 16)
-    order = [(r + d) % n for d in range(1, n + 1)]
+    g.wait_ge(S.ldb, 32)
+    rid, pid = topo.addr(base + 7, core)
+    g.remote_dma(T.xb[:], T.xb[:], S.got, S.snt, pid, rid, 0xFFFF)
     g.wait_ge(S.lda, 16)
     for i in range(0, n, 8):
-        g.remote_dma_fused([xfer(topo, core, T.cores[q] - 1, 1 << e, S.arr, [T.dh[q]], T.sd[r])
-                            for e, q in enumerate(order[i:i + 8])], local_sem=S.snt)
-    g.wait_ge(S.ldb, 32)
-    for i in range(0, n, 8):
-        g.remote_dma_fused([xfer(topo, core, T.cores[q] + 3, 1 << e, S.arr, [T.xs[:, b[q]:b[q] + 32]], T.slot[:, r, :])
+        g.remote_dma_fused([xfer(topo, core, T.cores[q] - 3 + a_core(q), 1 << e, S.arr, [T.dh[q]], T.sd[r])
                             for e, q in enumerate(order[i:i + 8])], local_sem=S.snt)
     if r == HOT:
         g.wait_ge(S.fin, 8 * n)
@@ -71,4 +83,4 @@ def rank_program(g, core, T, topo):
         g.wait_ge(S.fin, 8 * (w // 32))
         g.dma_start(T.y[:, 0:w], T.res[:, 0:w]).then_inc(S.acc, 16)
     g.wait_ge(S.acc, 16)
-    g.wait_ge(S.snt, 2 * n)
+    g.wait_ge(S.snt, n + 16)

@@ -1,30 +1,45 @@
 from concourse.bass import DstId, RemoteDMATransfer
 
 SCRATCH = {
-    "slot": ("sbuf", [128, 32, 32], "float32"),
     "xb": ("sbuf", [128, 1024], "float32"),
-    "res": ("sbuf", [128, 64], "float32"),
+    "xh": ("sbuf", [128, 128], "float32"),
     "dh": ("dram", [32, 128, 32], "float32"),
+    "ha": ("dram", [4, 128, 32], "float32"),
     "sd": ("dram", [32, 128, 32], "float32"),
     "f9": ("dram", [32, 128, 32], "float32"),
+    "rb": ("dram", [2, 128, 32], "float32"),
 }
-SEMAPHORES = ["lda", "ldb", "arr", "fin", "snt", "acc", "got"]
-HOT, WIDE = 9, 20
+SEMAPHORES = ["lda", "ldb", "ga", "gb", "arr", "fin", "snt", "acc"]
+HOT = 9
+P_CORES, M_CORES = (0, 1, 4, 5), (2, 3, 6, 7)
 
 
-def plan(widths):
-    n = len(widths)
-    off = [sum(widths[:r]) for r in range(n)]
-    b = [off[q] for q in range(n)]
-    bdst = [(q, 0) for q in range(n)]
-    b[HOT] = off[WIDE] + 32
-    bdst[HOT] = (WIDE, 32)
-    b = [o if o < off[HOT] else o - widths[HOT] for o in b]
-    return off, b, bdst
+def chip_of(t):
+    return 2 * t if t < 16 else 2 * (t - 16) + 1
+
+
+def unit_of(q):
+    return (q % 2) * 16 + q // 2
 
 
 def a_core(q):
-    return 2 if q % 4 < 2 else 6
+    return 2 if q // 8 < 2 else 6
+
+
+def chunks(c, p):
+    if c in P_CORES:
+        i, h = P_CORES.index(c), 4 * p
+    else:
+        i, h = M_CORES.index(c), 4 * (1 - p)
+    return h + i, h + (i + 2) % 4
+
+
+def b_owner(widths):
+    out = []
+    for q, w in enumerate(widths):
+        if q != HOT:
+            out += [(q, s) for s in range(w // 32)]
+    return out
 
 
 def xfer(topo, core, dst_core, mask, sem, srcs, dst):
@@ -35,7 +50,6 @@ def xfer(topo, core, dst_core, mask, sem, srcs, dst):
 
 def rank_program(g, core, T, topo):
     widths = T.tables["WIDTHS"]
-    off, b, bdst = plan(widths)
     n = len(widths)
     S = T.sem
     base = core - core % 8
@@ -43,44 +57,69 @@ def rank_program(g, core, T, topo):
     if r is None:
         return
     c = core % 8
-    order = [(r + d) % n for d in range(1, n + 1)]
-    if c in (2, 6):
-        g.wait_ge(S.arr, n)
-        if c == a_core(r):
-            t = xfer(topo, core, T.cores[HOT], 0xFF, S.fin, [T.sd[k] for k in range(n)], T.f9[r])
-        else:
-            q, col = bdst[r]
-            t = xfer(topo, core, T.cores[q], 0xFF, S.fin, [T.slot[:, k, :] for k in range(n)], T.res[:, col:col + 32])
-        g.remote_dma_fused([t], local_sem=S.snt)
-        g.wait_ge(S.snt, 8)
-        return
-    if c == 7:
-        g.wait_ge(S.got, 16)
-        for i in range(0, n, 8):
-            g.remote_dma_fused([xfer(topo, core, T.cores[q] - 3 + 8 - a_core(q), 1 << e, S.arr,
-                                     [T.xb[:, b[q]:b[q] + 32]], T.slot[:, r, :])
-                                for e, q in enumerate(order[i:i + 8])], local_sem=S.snt)
-        g.wait_ge(S.snt, n)
-        return
+    p = r % 2
+    ma, mb = chunks(c, p)
+    sent = 0
+
+    def send(kind, m, srcs):
+        ts = []
+        for j in range(4):
+            q = chip_of(4 * m + j)
+            rc = a_core(q) if kind == "a" else 8 - a_core(q)
+            ts.append(xfer(topo, core, T.cores[q] - 3 + rc, 3 << (2 * j), S.arr, [srcs[j]], T.sd[r]))
+        g.remote_dma_fused(ts, local_sem=S.snt)
+
     if c != 3:
+        g.wait_ge(S.ga, 4)
+        send("a", ma, [T.ha[j] for j in range(4)])
+        g.wait_ge(S.gb, 2)
+        send("b", mb, [T.xh[:, 32 * j:32 * j + 32] for j in range(4)])
+        sent += 16
+        if c in (2, 6):
+            g.wait_ge(S.arr, 2 * n)
+            srcs = [T.sd[k] for k in range(n)]
+            u = unit_of(r)
+            if c == a_core(r):
+                t = xfer(topo, core, T.cores[HOT], 0xFF, S.fin, srcs, T.f9[u])
+            else:
+                q, s = b_owner(widths)[u]
+                t = xfer(topo, core, T.cores[q], 0xFF, S.fin, srcs, T.rb[s])
+            g.remote_dma_fused([t], local_sem=S.snt)
+            sent += 8
+        g.wait_ge(S.snt, sent)
         return
-    h0, h1 = off[HOT], off[HOT] + widths[HOT]
+
+    h0 = sum(widths[:HOT])
+    h1 = h0 + widths[HOT]
+    g.dma_start(T.dh[:], T.x[:, h0:h1]).then_inc(S.lda, 16)
     g.dma_start(T.xb[:, 0:h0], T.x[:, 0:h0]).then_inc(S.ldb, 16)
     g.dma_start(T.xb[:, h0:], T.x[:, h1:]).then_inc(S.ldb, 16)
-    g.dma_start(T.dh[:], T.x[:, h0:h1]).then_inc(S.lda, 16)
-    g.wait_ge(S.ldb, 32)
-    rid, pid = topo.addr(base + 7, core)
-    g.remote_dma(T.xb[:], T.xb[:], S.got, S.snt, pid, rid, 0xFFFF)
+    others = [k for k in range(8) if k != 3]
     g.wait_ge(S.lda, 16)
-    for i in range(0, n, 8):
-        g.remote_dma_fused([xfer(topo, core, T.cores[q] - 3 + a_core(q), 1 << e, S.arr, [T.dh[q]], T.sd[r])
-                            for e, q in enumerate(order[i:i + 8])], local_sem=S.snt)
+    jobs = [(k, j) for j in range(4) for k in others]
+    for i in range(0, 28, 14):
+        g.remote_dma_fused([xfer(topo, core, base + k, 1 << e, S.ga, [T.dh[4 * chunks(k, p)[0] + j]], T.ha[j])
+                            for e, (k, j) in enumerate(jobs[i:i + 14])], local_sem=S.snt)
+    sent += 28
+    send("a", ma, [T.dh[4 * ma + j] for j in range(4)])
+    g.wait_ge(S.ldb, 32)
+    ts = []
+    for e, k in enumerate(others):
+        m = chunks(k, p)[1]
+        ts.append(xfer(topo, core, base + k, 3 << (2 * e), S.gb, [T.xb[:, 128 * m:128 * m + 128]], T.xh[:]))
+    g.remote_dma_fused(ts, local_sem=S.snt)
+    sent += 14
+    send("b", mb, [T.xb[:, 128 * mb + 32 * j:128 * mb + 32 * j + 32] for j in range(4)])
+    sent += 16
     if r == HOT:
         g.wait_ge(S.fin, 8 * n)
         g.dma_start(T.y[:, 0:1024], T.f9[:]).then_inc(S.acc, 16)
+        acc = 16
     else:
-        w = widths[r]
-        g.wait_ge(S.fin, 8 * (w // 32))
-        g.dma_start(T.y[:, 0:w], T.res[:, 0:w]).then_inc(S.acc, 16)
-    g.wait_ge(S.acc, 16)
-    g.wait_ge(S.snt, n + 16)
+        k = widths[r] // 32
+        g.wait_ge(S.fin, 8 * k)
+        for s in range(k):
+            g.dma_start(T.y[:, 32 * s:32 * s + 32], T.rb[s]).then_inc(S.acc, 16)
+        acc = 16 * k
+    g.wait_ge(S.acc, acc)
+    g.wait_ge(S.snt, sent)

@@ -4,34 +4,45 @@ SCRATCH = {
     "xb": ("sbuf", [128, 1024], "float32"),
     "xh": ("sbuf", [128, 128], "float32"),
     "dh": ("dram", [32, 128, 32], "float32"),
-    "ha": ("dram", [4, 128, 32], "float32"),
+    "ha": ("dram", [16, 128, 32], "float32"),
+    "de": ("dram", [8, 128, 4], "float32"),
     "sd": ("dram", [32, 128, 32], "float32"),
+    "se": ("dram", [32, 128, 4], "float32"),
     "f9": ("dram", [32, 128, 32], "float32"),
     "rb": ("dram", [2, 128, 32], "float32"),
+    "rr": ("dram", [8, 128, 4], "float32"),
 }
-SEMAPHORES = ["lda", "ldb", "ga", "gb", "arr", "fin", "snt", "acc"]
+SEMAPHORES = ["lda", "ldb", "lde", "ga", "gb", "arr", "are", "fin", "snt", "acc"]
 HOT = 9
+N = 32
 P_CORES, M_CORES = (0, 1, 4, 5), (2, 3, 6, 7)
-
-
-def chip_of(t):
-    return 2 * t if t < 16 else 2 * (t - 16) + 1
-
-
-def unit_of(q):
-    return (q % 2) * 16 + q // 2
+E_CHIPS = (2, 3, 10, 11, 18, 19, 26, 27)
+B_CHIPS = [2 * j for j in range(16)] + [q for q in range(1, N, 2) if q != HOT]
 
 
 def a_core(q):
-    return 2 if q // 8 < 2 else 6
+    return 2 if (q // 2) % 2 == 0 else 6
 
 
-def chunks(c, p):
+def sigma(r):
+    return (r // 2) % 2
+
+
+def a_lists(r):
+    u = [k for k in range(N) if sigma(k) == sigma(r)].index(r)
+    out = []
+    for s in (sigma(r), 1 - sigma(r)):
+        l = [q for q in range(N) if (q // 4) % 2 == s]
+        out.append(l[u:] + l[:u])
+    return out
+
+
+def b_chunk(c, r):
     if c in P_CORES:
-        i, h = P_CORES.index(c), 4 * p
+        i, h = P_CORES.index(c), 4 * (r % 2)
     else:
-        i, h = M_CORES.index(c), 4 * (1 - p)
-    return h + i, h + (i + 2) % 4
+        i, h = M_CORES.index(c), 4 * (1 - r % 2)
+    return h + (i + 2 * sigma(r)) % 4
 
 
 def b_owner(widths):
@@ -42,78 +53,86 @@ def b_owner(widths):
     return out
 
 
-def xfer(topo, core, dst_core, mask, sem, srcs, dst):
-    rid, pid = topo.addr(dst_core, core)
-    return RemoteDMATransfer(dst_ids=[DstId(rid=rid, pnc=pid)], dma_engine_mask=mask, remote_sem=sem,
-                             srcs=srcs, dsts=[dst], alu_op=1 if len(srcs) > 1 else 0)
-
-
 def rank_program(g, core, T, topo):
     widths = T.tables["WIDTHS"]
-    n = len(widths)
     S = T.sem
     base = core - core % 8
     r = T.rank_of(base + 3)
     if r is None:
         return
     c = core % 8
-    p = r % 2
-    ma, mb = chunks(c, p)
-    sent = 0
+    sent = [0]
+    e_rank, e_unit = b_owner(widths)[N - 1]
 
-    def send(kind, m, srcs):
-        ts = []
-        for j in range(4):
-            q = chip_of(4 * m + j)
-            rc = a_core(q) if kind == "a" else 8 - a_core(q)
-            ts.append(xfer(topo, core, T.cores[q] - 3 + rc, 3 << (2 * j), S.arr, [srcs[j]], T.sd[r]))
+    def xfer(dst_core, mask, sem, srcs, dst):
+        rid, pid = topo.addr(dst_core, core)
+        sent[0] += bin(mask).count("1")
+        return RemoteDMATransfer(dst_ids=[DstId(rid=rid, pnc=pid)], dma_engine_mask=mask, remote_sem=sem,
+                                 srcs=srcs, dsts=[dst], alu_op=1 if len(srcs) > 1 else 0)
+
+    def fused(ts):
         g.remote_dma_fused(ts, local_sem=S.snt)
 
+    def send_a(chips, src_of):
+        for i in range(0, 16, 8):
+            fused([xfer(T.cores[q] - 3 + a_core(q), 1 << e, S.arr, [src_of(i + e, q)], T.sd[r])
+                   for e, q in enumerate(chips[i:i + 8])])
+
+    def send_b(src_of):
+        m = b_chunk(c, r)
+        ts = []
+        for j in range(4):
+            if 4 * m + j < len(B_CHIPS):
+                q = B_CHIPS[4 * m + j]
+                ts.append(xfer(T.cores[q] - 3 + 8 - a_core(q), 3 << (2 * j), S.arr, [src_of(m, j)], T.sd[r]))
+        fused(ts)
+
+    direct, relay = a_lists(r)
     if c != 3:
-        g.wait_ge(S.ga, 4)
-        send("a", ma, [T.ha[j] for j in range(4)])
+        if c == 7:
+            g.wait_ge(S.ga, 16)
+            send_a(relay, lambda i, q: T.ha[i])
         g.wait_ge(S.gb, 2)
-        send("b", mb, [T.xh[:, 32 * j:32 * j + 32] for j in range(4)])
-        sent += 16
-        if c in (2, 6):
-            g.wait_ge(S.arr, 2 * n)
-            srcs = [T.sd[k] for k in range(n)]
-            u = unit_of(r)
-            if c == a_core(r):
-                t = xfer(topo, core, T.cores[HOT], 0xFF, S.fin, srcs, T.f9[u])
-            else:
-                q, s = b_owner(widths)[u]
-                t = xfer(topo, core, T.cores[q], 0xFF, S.fin, srcs, T.rb[s])
-            g.remote_dma_fused([t], local_sem=S.snt)
-            sent += 8
-        g.wait_ge(S.snt, sent)
+        send_b(lambda m, j: T.xh[:, 32 * j:32 * j + 32])
+        if c == a_core(r):
+            g.wait_ge(S.arr, N)
+            fused([xfer(T.cores[HOT], 0xFF, S.fin, [T.sd[k] for k in range(N)], T.f9[r])])
+        elif c == 8 - a_core(r) and r != HOT:
+            g.wait_ge(S.arr, 2 * N)
+            q, s = b_owner(widths)[B_CHIPS.index(r)]
+            fused([xfer(T.cores[q], 0xFF, S.fin, [T.sd[k] for k in range(N)], T.rb[s])])
+        elif c == 7 and r in E_CHIPS:
+            g.wait_ge(S.are, N)
+            fused([xfer(T.cores[e_rank], 0x0F, S.fin, [T.se[k] for k in range(N)], T.rr[E_CHIPS.index(r)])])
+        g.wait_ge(S.snt, sent[0])
         return
 
     h0 = sum(widths[:HOT])
     h1 = h0 + widths[HOT]
+    e0 = sum(widths[:e_rank]) + 32 * e_unit
     g.dma_start(T.dh[:], T.x[:, h0:h1]).then_inc(S.lda, 16)
     g.dma_start(T.xb[:, 0:h0], T.x[:, 0:h0]).then_inc(S.ldb, 16)
     g.dma_start(T.xb[:, h0:], T.x[:, h1:]).then_inc(S.ldb, 16)
-    others = [k for k in range(8) if k != 3]
+    g.dma_start(T.de[:], T.x[:, e0:e0 + 32]).then_inc(S.lde, 16)
     g.wait_ge(S.lda, 16)
-    jobs = [(k, j) for j in range(4) for k in others]
-    for i in range(0, 28, 14):
-        g.remote_dma_fused([xfer(topo, core, base + k, 1 << e, S.ga, [T.dh[4 * chunks(k, p)[0] + j]], T.ha[j])
-                            for e, (k, j) in enumerate(jobs[i:i + 14])], local_sem=S.snt)
-    sent += 28
-    send("a", ma, [T.dh[4 * ma + j] for j in range(4)])
+    fused([xfer(base + 7, 1 << e, S.ga, [T.dh[q]], T.ha[e]) for e, q in enumerate(relay)])
+    send_a(direct, lambda i, q: T.dh[q])
     g.wait_ge(S.ldb, 32)
     ts = []
-    for e, k in enumerate(others):
-        m = chunks(k, p)[1]
-        ts.append(xfer(topo, core, base + k, 3 << (2 * e), S.gb, [T.xb[:, 128 * m:128 * m + 128]], T.xh[:]))
-    g.remote_dma_fused(ts, local_sem=S.snt)
-    sent += 14
-    send("b", mb, [T.xb[:, 128 * mb + 32 * j:128 * mb + 32 * j + 32] for j in range(4)])
-    sent += 16
+    for e, k in enumerate(k for k in range(8) if k != 3):
+        m = b_chunk(k, r)
+        ts.append(xfer(base + k, 3 << (2 * e), S.gb, [T.xb[:, 128 * m:128 * m + 128]], T.xh[:]))
+    fused(ts)
+    send_b(lambda m, j: T.xb[:, 128 * m + 32 * j:128 * m + 32 * j + 32])
+    g.wait_ge(S.lde, 16)
+    fused([xfer(T.cores[q] + 4, 1 << e, S.are, [T.de[e]], T.se[r]) for e, q in enumerate(E_CHIPS)])
     if r == HOT:
-        g.wait_ge(S.fin, 8 * n)
+        g.wait_ge(S.fin, 8 * N)
         g.dma_start(T.y[:, 0:1024], T.f9[:]).then_inc(S.acc, 16)
+        acc = 16
+    elif r == e_rank:
+        g.wait_ge(S.fin, 4 * 8)
+        g.dma_start(T.y[:, 0:32], T.rr[:]).then_inc(S.acc, 16)
         acc = 16
     else:
         k = widths[r] // 32
@@ -122,4 +141,4 @@ def rank_program(g, core, T, topo):
             g.dma_start(T.y[:, 32 * s:32 * s + 32], T.rb[s]).then_inc(S.acc, 16)
         acc = 16 * k
     g.wait_ge(S.acc, acc)
-    g.wait_ge(S.snt, sent)
+    g.wait_ge(S.snt, sent[0])

from concourse.bass import DstId, RemoteDMATransfer

SCRATCH = {
    "xb": ("sbuf", [128, 1024], "float32"),
    "xh": ("sbuf", [128, 128], "float32"),
    "dh": ("dram", [32, 128, 32], "float32"),
    "ha": ("dram", [16, 128, 32], "float32"),
    "de": ("dram", [8, 128, 4], "float32"),
    "sd": ("dram", [32, 128, 32], "float32"),
    "se": ("dram", [32, 128, 4], "float32"),
    "f9": ("dram", [32, 128, 32], "float32"),
    "rb": ("dram", [2, 128, 32], "float32"),
    "rr": ("dram", [8, 128, 4], "float32"),
}
SEMAPHORES = ["lda", "ldb", "lde", "ga", "gb", "arr", "are", "fin", "snt", "acc"]
HOT = 9
N = 32
P_CORES, M_CORES = (0, 1, 4, 5), (2, 3, 6, 7)
E_CHIPS = (2, 3, 10, 11, 18, 19, 26, 27)
B_CHIPS = [2 * j for j in range(16)] + [q for q in range(1, N, 2) if q != HOT]


def a_core(q):
    return 2 if (q // 2) % 2 == 0 else 6


def sigma(r):
    return (r // 2) % 2


def a_lists(r):
    u = [k for k in range(N) if sigma(k) == sigma(r)].index(r)
    out = []
    for s in (sigma(r), 1 - sigma(r)):
        l = [q for q in range(N) if (q // 4) % 2 == s]
        out.append(l[u:] + l[:u])
    return out


def b_chunk(c, r):
    if c in P_CORES:
        i, h = P_CORES.index(c), 4 * (r % 2)
    else:
        i, h = M_CORES.index(c), 4 * (1 - r % 2)
    return h + (i + 2 * sigma(r)) % 4


def b_owner(widths):
    out = []
    for q, w in enumerate(widths):
        if q != HOT:
            out += [(q, s) for s in range(w // 32)]
    return out


def rank_program(g, core, T, topo):
    widths = T.tables["WIDTHS"]
    S = T.sem
    base = core - core % 8
    r = T.rank_of(base + 3)
    if r is None:
        return
    c = core % 8
    sent = [0]
    e_rank, e_unit = b_owner(widths)[N - 1]

    def xfer(dst_core, mask, sem, srcs, dst):
        rid, pid = topo.addr(dst_core, core)
        sent[0] += bin(mask).count("1")
        return RemoteDMATransfer(dst_ids=[DstId(rid=rid, pnc=pid)], dma_engine_mask=mask, remote_sem=sem,
                                 srcs=srcs, dsts=[dst], alu_op=1 if len(srcs) > 1 else 0)

    def fused(ts):
        g.remote_dma_fused(ts, local_sem=S.snt)

    def send_a(chips, src_of):
        for i in range(0, 16, 8):
            fused([xfer(T.cores[q] - 3 + a_core(q), 1 << e, S.arr, [src_of(i + e, q)], T.sd[r])
                   for e, q in enumerate(chips[i:i + 8])])

    def send_b(src_of):
        m = b_chunk(c, r)
        ts = []
        for j in range(4):
            if 4 * m + j < len(B_CHIPS):
                q = B_CHIPS[4 * m + j]
                ts.append(xfer(T.cores[q] - 3 + 8 - a_core(q), 3 << (2 * j), S.arr, [src_of(m, j)], T.sd[r]))
        fused(ts)

    direct, relay = a_lists(r)
    if c != 3:
        if c == 7:
            g.wait_ge(S.ga, 16)
            send_a(relay, lambda i, q: T.ha[i])
        g.wait_ge(S.gb, 2)
        send_b(lambda m, j: T.xh[:, 32 * j:32 * j + 32])
        if c == a_core(r):
            g.wait_ge(S.arr, N)
            fused([xfer(T.cores[HOT], 0xFF, S.fin, [T.sd[k] for k in range(N)], T.f9[r])])
        elif c == 8 - a_core(r) and r != HOT:
            g.wait_ge(S.arr, 2 * N)
            q, s = b_owner(widths)[B_CHIPS.index(r)]
            fused([xfer(T.cores[q], 0xFF, S.fin, [T.sd[k] for k in range(N)], T.rb[s])])
        elif c == 7 and r in E_CHIPS:
            g.wait_ge(S.are, N)
            fused([xfer(T.cores[e_rank], 0x0F, S.fin, [T.se[k] for k in range(N)], T.rr[E_CHIPS.index(r)])])
        g.wait_ge(S.snt, sent[0])
        return

    h0 = sum(widths[:HOT])
    h1 = h0 + widths[HOT]
    e0 = sum(widths[:e_rank]) + 32 * e_unit
    g.dma_start(T.dh[:], T.x[:, h0:h1]).then_inc(S.lda, 16)
    g.dma_start(T.xb[:, 0:h0], T.x[:, 0:h0]).then_inc(S.ldb, 16)
    g.dma_start(T.xb[:, h0:], T.x[:, h1:]).then_inc(S.ldb, 16)
    g.dma_start(T.de[:], T.x[:, e0:e0 + 32]).then_inc(S.lde, 16)
    g.wait_ge(S.lda, 16)
    fused([xfer(base + 7, 1 << e, S.ga, [T.dh[q]], T.ha[e]) for e, q in enumerate(relay)])
    send_a(direct, lambda i, q: T.dh[q])
    g.wait_ge(S.ldb, 32)
    ts = []
    for e, k in enumerate(k for k in range(8) if k != 3):
        m = b_chunk(k, r)
        ts.append(xfer(base + k, 3 << (2 * e), S.gb, [T.xb[:, 128 * m:128 * m + 128]], T.xh[:]))
    fused(ts)
    send_b(lambda m, j: T.xb[:, 128 * m + 32 * j:128 * m + 32 * j + 32])
    g.wait_ge(S.lde, 16)
    fused([xfer(T.cores[q] + 4, 1 << e, S.are, [T.de[e]], T.se[r]) for e, q in enumerate(E_CHIPS)])
    if r == HOT:
        g.wait_ge(S.fin, 8 * N)
        g.dma_start(T.y[:, 0:1024], T.f9[:]).then_inc(S.acc, 16)
        acc = 16
    elif r == e_rank:
        g.wait_ge(S.fin, 4 * 8)
        g.dma_start(T.y[:, 0:32], T.rr[:]).then_inc(S.acc, 16)
        acc = 16
    else:
        k = widths[r] // 32
        g.wait_ge(S.fin, 8 * k)
        for s in range(k):
            g.dma_start(T.y[:, 32 * s:32 * s + 32], T.rb[s]).then_inc(S.acc, 16)
        acc = 16 * k
    g.wait_ge(S.acc, acc)
    g.wait_ge(S.snt, sent[0])
